import numpy as np
import ml_dtypes


def mxq(x, axis, fmt="e4m3"):
    dtype, down = {"e4m3": (ml_dtypes.float8_e4m3fn, 7), "e5m2": (ml_dtypes.float8_e5m2, 14)}[fmt]
    v = np.moveaxis(np.asarray(x, np.float32).astype(ml_dtypes.bfloat16).astype(np.float64), axis, -1)
    blocks = v.reshape(v.shape[:-1] + (-1, 32))
    amax = np.abs(blocks).max(-1, keepdims=True)
    byte = np.maximum(np.where(amax > 0, np.frexp(amax)[1] - 1 + 127, 0) - down, 1)
    scale = np.exp2(byte - 127.0)
    codes = (blocks / scale).astype(np.float32).astype(dtype).astype(np.float64)
    return np.moveaxis((codes * scale).reshape(v.shape), -1, axis)


WIDE = False


def mx_kscale(k):
    if not WIDE:
        return np.ones(k)
    levels = np.array([10, -10, 5, -5, 0])
    if k % 512:
        return np.exp2(np.random.permutation(np.resize(levels, k // 32))).repeat(32)
    a = np.empty((k // 512, 16))
    for p in range(k // 512):
        a[p, :8] = np.random.permutation(np.resize(levels, 8))
        for g in range(8):
            far = levels[np.abs(levels - a[p, g]) >= 10]
            a[p, g + 8] = far[np.random.randint(len(far))]
    return np.exp2(a.ravel()).repeat(32)


def f64(x):
    return np.asarray(x).astype(np.float64)


def striped(idx):
    return np.tile(np.asarray(idx).reshape(-1, 16).T, (8, 1)).astype(np.uint16)


def unstriped(offs):
    return offs[:16].T.reshape(-1).astype(np.int64)


E2M1 = np.array([0.0, 0.5, 1.0, 1.5, 2.0, 3.0, 4.0, 6.0, -0.0, -0.5, -1.0, -1.5, -2.0, -3.0, -4.0, -6.0])


def pack_weight(w, fmt):
    k, n = w.shape
    w = f64(np.asarray(w, np.float32).astype(ml_dtypes.bfloat16)).reshape(k // 32, 32, n)
    amax = np.abs(w).max(1)
    if fmt == "e4m3":
        byte = np.frexp(amax)[1] - 1 + 127 - 7
    else:
        mant, ex = np.frexp(amax / 6.0)
        byte = np.where(mant > 0.5, ex, ex - 1) + 127
    byte = np.clip(np.where(amax > 0, byte, 1), 1, 254)
    scaled = (w * np.exp2(127.0 - byte)[:, None, :]).reshape(k, n).astype(np.float32)
    by_word = np.ascontiguousarray(scaled.reshape(k // 512, 128, 4, n).transpose(0, 1, 3, 2))
    if fmt == "e4m3":
        words = by_word.astype(ml_dtypes.float8_e4m3fn).view(np.uint8)
    else:
        c = by_word.astype(ml_dtypes.float4_e2m1fn).view(np.uint8) & 0xF
        words = (c[..., 0::2] | (c[..., 1::2] << 4)).reshape(k // 512, 128, 2 * n)
    return np.ascontiguousarray(words), np.ascontiguousarray(byte.astype(np.uint8).reshape(k // 512, 16, n))


def unpack_weight(words, scales, fmt):
    g, _, n = scales.shape
    words = np.ascontiguousarray(words).reshape(g, 128, n, -1)
    if fmt == "e4m3":
        vals = words.view(ml_dtypes.float8_e4m3fn).astype(np.float64)
    else:
        nib = np.empty((g, 128, n, 4), np.uint8)
        nib[..., 0::2] = words & 0xF
        nib[..., 1::2] = words >> 4
        vals = E2M1[nib]
    vals = vals * np.repeat(np.exp2(scales.astype(np.float64) - 127.0), 8, axis=1)[..., None]
    return vals.transpose(0, 1, 3, 2).reshape(g * 512, n)


D, E, T, I, Q = 512, 512, 2048, 512, 128


def setup_inputs():
    n = np.random.standard_normal
    idx = np.random.permutation(T)[:I]
    fd = mx_kscale(D)
    fe = mx_kscale(E)
    keysp = pack_weight(n((D, T)) / fd[:, None], "e4m3")
    valsp = pack_weight(n((E, T)) / fe[:, None], "e4m3")
    return {
        "query": (n((D, Q)) * 1.0 / np.sqrt(D) * fd[:, None]).astype(np.float32),
        "keys_words": keysp[0],
        "keys_scales": keysp[1],
        "aim": (np.random.uniform(0.5, 2.0, (Q, 1))).astype(np.float32),
        "soft": (np.random.uniform(0.5, 2.0, (Q, 1))).astype(np.float32),
        "gout": (n((E, Q)) * 1 / np.sqrt(E) * fe[:, None]).astype(np.float32),
        "vals_words": valsp[0],
        "vals_scales": valsp[1],
        "old": (0.5 * n((Q, T))).astype(np.float32),
        "offs": striped(idx),
    }


def reference(query, keys_words, keys_scales, aim, soft, gout, vals_words, vals_scales, old, offs):
    idx = unstriped(offs)
    keysu = unpack_weight(keys_words, keys_scales, "e4m3")
    valsu = unpack_weight(vals_words, vals_scales, "e4m3")
    queryq = mxq(f64(query), 0, "e4m3")
    keysidxg = keysu[:, idx]
    a = queryq.T @ keysidxg
    p = 1.0 / (np.square(f64(aim) - a) + f64(soft))
    z = np.sum(p, axis=1, keepdims=True)
    goutq = mxq(f64(gout), 0, "e4m3")
    valsidxg = valsu[:, idx]
    c0 = goutq.T @ valsidxg
    dz = np.sum(c0 * p / np.square(z) * (-1.0), axis=1, keepdims=True)
    dp = c0 / z + dz
    da = dp * (-1.0) / np.square(np.square(f64(aim) - a) + f64(soft)) * (f64(aim) - a) * 2.0 * (-1.0)
    gs = da * 512.0
    gf = np.zeros((Q, T))
    gf[:, idx] = gs
    y = f64(old) + gf
    return y

@@ -1,0 +1,150 @@
+from contextlib import ExitStack
+
+import concourse.mybir as mybir
+from concourse.masks import make_identity
+
+D, E, T, I, Q = 512, 512, 2048, 512, 128
+FLOPS = 2 * Q * I * (D + E)
+
+F32 = mybir.dt.float32
+BF16 = mybir.dt.bfloat16
+I32 = mybir.dt.int32
+U32 = mybir.dt.uint32
+U16 = mybir.dt.uint16
+U8 = mybir.dt.uint8
+FP8X4 = mybir.dt.float8_e4m3fn_x4
+ALU = mybir.AluOpType
+ACT = mybir.ActivationFunctionType
+
+P = 128
+PACK = 4
+H = I // 2
+VAL_ROW = 4
+OUT_COLS = (256, 512, 512, 512, 256)
+
+
+def tile_attend_bnearpoint_s_kernel(tc, query, keys_words, keys_scales, aim, soft, gout, vals_words, vals_scales, old, offs, out):
+    nc = tc.nc
+    with ExitStack() as ctx:
+        sb = ctx.enter_context(tc.tile_pool(name="sb", bufs=1))
+        ps = ctx.enter_context(tc.psum_pool(name="ps", bufs=1))
+
+        offsets = sb.tile([P, I // 16], U16, name="offsets")
+        key_bytes = sb.tile([P, T], U8, name="key_bytes")
+        val_bytes = sb.tile([P, T], U8, name="val_bytes")
+        key_words = sb.tile([P, T], I32, name="key_words")
+        val_words = sb.tile([P, T], I32, name="val_words", tag="val_words")
+        q_raw = sb.tile([P, PACK, Q], F32, name="q_raw")
+        g_raw = sb.tile([P, PACK, Q], F32, name="g_raw")
+        aim_sb = sb.tile([P, 1], F32, name="aim_sb")
+        soft_sb = sb.tile([P, 1], F32, name="soft_sb")
+        old_sb = sb.tile([P, T], F32, name="old_sb")
+        placed = sb.tile([P, T], F32, name="placed")
+
+        one = sb.tile([P, 1], F32, name="one")
+        for plane in (key_bytes, val_bytes):
+            nc.vector.memset(plane[:, 0 : T // 2].bitcast(I32), 0)
+            nc.gpsimd.memset(plane[:, T // 2 : T].bitcast(I32), 0)
+        nc.vector.memset(one[:], 1.0)
+        nc.vector.memset(placed[:], 0.0)
+        ident = sb.tile([P, P], F32, name="ident")
+        make_identity(nc, ident[:])
+
+        def load_bytes(engine, plane, scales, row):
+            for quad in range(4):
+                engine.dma_start(
+                    out=plane[32 * quad + row : 32 * quad + row + 4, :].bitcast(I32),
+                    in_=scales[0, 4 * quad : 4 * quad + 4, :].bitcast(I32),
+                )
+
+        def words_of(ap):
+            return ap[0].rearrange("p n t -> p (n t)").bitcast(I32)
+
+        nc.sync.dma_start(offsets[:], offs)
+        nc.sync.dma_start(out=q_raw[:], in_=query.rearrange("(p j) w -> p j w", j=PACK))
+        nc.sync.dma_start(out=g_raw[:], in_=gout.rearrange("(p j) w -> p j w", j=PACK))
+        load_bytes(nc.sync, key_bytes, keys_scales, 0)
+        nc.sync.dma_start(out=key_words[:], in_=words_of(keys_words))
+        load_bytes(nc.sync, val_bytes, vals_scales, VAL_ROW)
+        nc.sync.dma_start(out=aim_sb[:], in_=aim)
+        nc.sync.dma_start(out=soft_sb[:], in_=soft)
+        nc.sync.dma_start(out=val_words[:], in_=words_of(vals_words))
+        nc.sync.dma_start(out=old_sb[:], in_=old)
+
+        def quantise(raw, name):
+            woven = sb.tile([P, Q, PACK], BF16, name=name + "_woven", align_bytes=64)
+            codes = sb.tile([P, Q], U32, name=name + "_codes", align_bytes=64)
+            scales = sb.tile([P, Q], U8, name=name + "_scales", align_bytes=64)
+            nc.scalar.copy(out=woven[:], in_=raw[:].rearrange("p j w -> p w j"))
+            nc.vector.quantize_mx(out=codes[:].bitcast(FP8X4), scales=scales[:], in_=woven[:].rearrange("p w j -> p (w j)"))
+            return codes, scales
+
+        def gather_bytes(plane, name):
+            got = sb.tile([P, I], U8, name=name, align_bytes=64)
+            nc.vector.tensor_copy(got[:], plane[:].indirect(offsets[:]))
+            return got
+
+        def product(stat, words, got_bytes, row, h, name):
+            got = sb.tile([P, H], U32, name=name + "_got%d" % h, align_bytes=64)
+            nc.vector.tensor_copy(got[:], words[:].bitcast(U32).indirect(offsets[:, h * H // 16 : (h + 1) * H // 16]))
+            acc = ps.tile([P, I], F32, name=name + "_acc%d" % h)
+            if name == "c" and h == 1:
+                nc.tensor.transpose(acc[:, H : H + P], one[:].to_broadcast([P, P]), ident[:])
+            nc.tensor.matmul_mx(
+                out=acc[:, 0:H],
+                lhsT=stat[0][:].bitcast(FP8X4),
+                lhsT_scale=stat[1][:],
+                rhs=got[:].bitcast(FP8X4),
+                rhs_scale=got_bytes[row:P, h * H : (h + 1) * H],
+                start=True,
+                stop=True,
+            )
+            return acc
+
+        kb = gather_bytes(key_bytes, "kb")
+        qq = quantise(q_raw, "q")
+        gq = quantise(g_raw, "g")
+        a = [product(qq, key_words, kb, 0, h, "a") for h in range(2)]
+        vb = gather_bytes(val_bytes, "vb")
+
+        def half_tiles(name):
+            return [sb.tile([P, H + 8], F32, name=name + "%d" % h) for h in range(2)]
+
+        def column(name):
+            return sb.tile([P, 1], F32, name=name)
+
+        sq, root, part, part2 = half_tiles("sq"), half_tiles("root"), half_tiles("part"), half_tiles("part2")
+        z = [column("z0"), column("z1")]
+        for h in range(2):
+            nc.scalar.activation(sq[h][:, 0:H], a[h][:, 0:H], ACT.Square, bias=aim_sb[:], scale=-1.0)
+        for h in range(2):
+            nc.scalar.activation(root[h][:, 0:H], sq[h][:, 0:H], ACT.Abs_reciprocal_sqrt, bias=soft_sb[:])
+        for h in range(2):
+            nc.scalar.activation(part[h][:, 0:H], root[h][:, 0:H], ACT.Square, accum_out=z[h][:])
+        z_all, neg_rz, rz2, shift = column("z_all"), column("neg_rz"), column("rz2"), column("shift")
+        nc.scalar.activation(z_all[:], z[0][:], ACT.Identity, bias=z[1][:])
+        for h in range(2):
+            nc.scalar.activation(part2[h][:, 0:H], part[h][:, 0:H], ACT.Square, scale=32.0)
+        c0 = [product(gq, val_words, vb, VAL_ROW, h, "c") for h in range(2)]
+        late = sb.tile([P, I + 8], F32, name="late", tag="val_words")
+        rz = late[:, I : I + 1]
+        nc.vector.reciprocal(rz, z_all[:])
+        nc.scalar.activation(rz2[:], rz, ACT.Square)
+        nc.scalar.activation(neg_rz[:], rz, ACT.Copy, scale=-1.0)
+        cp = half_tiles("cp")
+        dp = sb.tile([P, I], F32, name="dp")
+        nc.vector.scalar_tensor_tensor(cp[0][:, 0:H], c0[0][:, 0:H], 1.0, part[0][:, 0:H], ALU.mult, ALU.mult, accum_out=part[1][:, H : H + 1])
+        nc.vector.scalar_tensor_tensor(late[:, 0:H], a[0][:, 0:H], aim_sb[:], part2[0][:, 0:H], ALU.subtract, ALU.mult)
+        nc.vector.scalar_tensor_tensor(cp[1][:, 0 : H + 1], c0[1][:, 0 : H + 1], rz2[:], part[1][:, 0 : H + 1], ALU.mult, ALU.mult, accum_out=shift[:])
+        nc.vector.scalar_tensor_tensor(late[:, H:I], a[1][:, 0:H], aim_sb[:], part2[1][:, 0:H], ALU.subtract, ALU.mult)
+        nc.vector.tensor_scalar(dp[:, 0:H], c0[0][:, 0:H], neg_rz[:], shift[:], ALU.mult, ALU.add)
+        nc.scalar.activation(dp[:, H:I], c0[1][:, 0:H], ACT.Identity, bias=shift[:], scale=neg_rz[:])
+        nc.vector.tensor_tensor(placed[:].indirect(offsets[:]), dp[:], late[:, 0:I], ALU.mult)
+
+        t0 = 0
+        for n, width in enumerate(OUT_COLS):
+            cols = slice(t0, t0 + width)
+            res = sb.tile([P, width], F32, name="res%d" % n)
+            nc.vector.tensor_tensor(res[:], placed[:, cols], old_sb[:, cols], ALU.add)
+            (nc.sync if n % 2 == 0 else nc.scalar).dma_start(out=out[:, cols], in_=res[:])
+            t0 += width

@@ -42,19 +42,21 @@ def tile_attend_bnearpoint_s_kernel(tc, query, keys_words, keys_scales, aim, sof
         placed = sb.tile([P, T], F32, name="placed")
 
         one = sb.tile([P, 1], F32, name="one")
+        warm = sb.tile([P, 1], F32, name="warm")
         for plane in (key_bytes, val_bytes):
             nc.vector.memset(plane[:, 0 : T // 2].bitcast(I32), 0)
             nc.gpsimd.memset(plane[:, T // 2 : T].bitcast(I32), 0)
         nc.vector.memset(one[:], 1.0)
+        nc.scalar.activation(warm[:], one[:], ACT.Abs_reciprocal_sqrt)
         nc.vector.memset(placed[:], 0.0)
         ident = sb.tile([P, P], F32, name="ident")
         make_identity(nc, ident[:])
 
         def load_bytes(engine, plane, scales, row):
-            for quad in range(4):
+            for r in range(4):
                 engine.dma_start(
-                    out=plane[32 * quad + row : 32 * quad + row + 4, :].bitcast(I32),
-                    in_=scales[0, 4 * quad : 4 * quad + 4, :].bitcast(I32),
+                    out=plane[row + r : P : 32, :].bitcast(I32),
+                    in_=scales[0, r:16:4, :].bitcast(I32),
                 )
 
         def words_of(ap):

@@ -44,8 +44,7 @@ def tile_attend_bnearpoint_s_kernel(tc, query, keys_words, keys_scales, aim, sof
         one = sb.tile([P, 1], F32, name="one")
         warm = sb.tile([P, 1], F32, name="warm")
         for plane in (key_bytes, val_bytes):
-            nc.vector.memset(plane[:, 0 : T // 2].bitcast(I32), 0)
-            nc.gpsimd.memset(plane[:, T // 2 : T].bitcast(I32), 0)
+            nc.vector.memset(plane[:].bitcast(I32), 0)
         nc.vector.memset(one[:], 1.0)
         nc.scalar.activation(warm[:], one[:], ACT.Abs_reciprocal_sqrt)
         nc.vector.memset(placed[:], 0.0)

from contextlib import ExitStack

import concourse.mybir as mybir
from concourse.masks import make_identity

D, E, T, I, Q = 512, 512, 2048, 512, 128
FLOPS = 2 * Q * I * (D + E)

F32 = mybir.dt.float32
BF16 = mybir.dt.bfloat16
I32 = mybir.dt.int32
U32 = mybir.dt.uint32
U16 = mybir.dt.uint16
U8 = mybir.dt.uint8
FP8X4 = mybir.dt.float8_e4m3fn_x4
ALU = mybir.AluOpType
ACT = mybir.ActivationFunctionType

P = 128
PACK = 4
H = I // 2
VAL_ROW = 4
OUT_COLS = (256, 512, 512, 512, 256)


def tile_attend_bnearpoint_s_kernel(tc, query, keys_words, keys_scales, aim, soft, gout, vals_words, vals_scales, old, offs, out):
    nc = tc.nc
    with ExitStack() as ctx:
        sb = ctx.enter_context(tc.tile_pool(name="sb", bufs=1))
        ps = ctx.enter_context(tc.psum_pool(name="ps", bufs=1))

        offsets = sb.tile([P, I // 16], U16, name="offsets")
        key_bytes = sb.tile([P, T], U8, name="key_bytes")
        val_bytes = sb.tile([P, T], U8, name="val_bytes")
        key_words = sb.tile([P, T], I32, name="key_words")
        val_words = sb.tile([P, T], I32, name="val_words", tag="val_words")
        q_raw = sb.tile([P, PACK, Q], F32, name="q_raw")
        g_raw = sb.tile([P, PACK, Q], F32, name="g_raw")
        aim_sb = sb.tile([P, 1], F32, name="aim_sb")
        soft_sb = sb.tile([P, 1], F32, name="soft_sb")
        old_sb = sb.tile([P, T], F32, name="old_sb")
        placed = sb.tile([P, T], F32, name="placed")

        one = sb.tile([P, 1], F32, name="one")
        warm = sb.tile([P, 1], F32, name="warm")
        for plane in (key_bytes, val_bytes):
            nc.vector.memset(plane[:].bitcast(I32), 0)
        nc.vector.memset(one[:], 1.0)
        nc.scalar.activation(warm[:], one[:], ACT.Abs_reciprocal_sqrt)
        nc.vector.memset(placed[:], 0.0)
        ident = sb.tile([P, P], F32, name="ident")
        make_identity(nc, ident[:])

        def load_bytes(engine, plane, scales, row):
            for r in range(4):
                engine.dma_start(
                    out=plane[row + r : P : 32, :].bitcast(I32),
                    in_=scales[0, r:16:4, :].bitcast(I32),
                )

        def words_of(ap):
            return ap[0].rearrange("p n t -> p (n t)").bitcast(I32)

        nc.sync.dma_start(offsets[:], offs)
        nc.sync.dma_start(out=q_raw[:], in_=query.rearrange("(p j) w -> p j w", j=PACK))
        nc.sync.dma_start(out=g_raw[:], in_=gout.rearrange("(p j) w -> p j w", j=PACK))
        load_bytes(nc.sync, key_bytes, keys_scales, 0)
        nc.sync.dma_start(out=key_words[:], in_=words_of(keys_words))
        load_bytes(nc.sync, val_bytes, vals_scales, VAL_ROW)
        nc.sync.dma_start(out=aim_sb[:], in_=aim)
        nc.sync.dma_start(out=soft_sb[:], in_=soft)
        nc.sync.dma_start(out=val_words[:], in_=words_of(vals_words))
        nc.sync.dma_start(out=old_sb[:], in_=old)

        def quantise(raw, name):
            woven = sb.tile([P, Q, PACK], BF16, name=name + "_woven", align_bytes=64)
            codes = sb.tile([P, Q], U32, name=name + "_codes", align_bytes=64)
            scales = sb.tile([P, Q], U8, name=name + "_scales", align_bytes=64)
            nc.scalar.copy(out=woven[:], in_=raw[:].rearrange("p j w -> p w j"))
            nc.vector.quantize_mx(out=codes[:].bitcast(FP8X4), scales=scales[:], in_=woven[:].rearrange("p w j -> p (w j)"))
            return codes, scales

        def gather_bytes(plane, name):
            got = sb.tile([P, I], U8, name=name, align_bytes=64)
            nc.vector.tensor_copy(got[:], plane[:].indirect(offsets[:]))
            return got

        def product(stat, words, got_bytes, row, h, name):
            got = sb.tile([P, H], U32, name=name + "_got%d" % h, align_bytes=64)
            nc.vector.tensor_copy(got[:], words[:].bitcast(U32).indirect(offsets[:, h * H // 16 : (h + 1) * H // 16]))
            acc = ps.tile([P, I], F32, name=name + "_acc%d" % h)
            if name == "c" and h == 1:
                nc.tensor.transpose(acc[:, H : H + P], one[:].to_broadcast([P, P]), ident[:])
            nc.tensor.matmul_mx(
                out=acc[:, 0:H],
                lhsT=stat[0][:].bitcast(FP8X4),
                lhsT_scale=stat[1][:],
                rhs=got[:].bitcast(FP8X4),
                rhs_scale=got_bytes[row:P, h * H : (h + 1) * H],
                start=True,
                stop=True,
            )
            return acc

        kb = gather_bytes(key_bytes, "kb")
        qq = quantise(q_raw, "q")
        gq = quantise(g_raw, "g")
        a = [product(qq, key_words, kb, 0, h, "a") for h in range(2)]
        vb = gather_bytes(val_bytes, "vb")

        def half_tiles(name):
            return [sb.tile([P, H + 8], F32, name=name + "%d" % h) for h in range(2)]

        def column(name):
            return sb.tile([P, 1], F32, name=name)

        sq, root, part, part2 = half_tiles("sq"), half_tiles("root"), half_tiles("part"), half_tiles("part2")
        z = [column("z0"), column("z1")]
        for h in range(2):
            nc.scalar.activation(sq[h][:, 0:H], a[h][:, 0:H], ACT.Square, bias=aim_sb[:], scale=-1.0)
        for h in range(2):
            nc.scalar.activation(root[h][:, 0:H], sq[h][:, 0:H], ACT.Abs_reciprocal_sqrt, bias=soft_sb[:])
        for h in range(2):
            nc.scalar.activation(part[h][:, 0:H], root[h][:, 0:H], ACT.Square, accum_out=z[h][:])
        z_all, neg_rz, rz2, shift = column("z_all"), column("neg_rz"), column("rz2"), column("shift")
        nc.scalar.activation(z_all[:], z[0][:], ACT.Identity, bias=z[1][:])
        for h in range(2):
            nc.scalar.activation(part2[h][:, 0:H], part[h][:, 0:H], ACT.Square, scale=32.0)
        c0 = [product(gq, val_words, vb, VAL_ROW, h, "c") for h in range(2)]
        late = sb.tile([P, I + 8], F32, name="late", tag="val_words")
        rz = late[:, I : I + 1]
        nc.vector.reciprocal(rz, z_all[:])
        nc.scalar.activation(rz2[:], rz, ACT.Square)
        nc.scalar.activation(neg_rz[:], rz, ACT.Copy, scale=-1.0)
        cp = half_tiles("cp")
        dp = sb.tile([P, I], F32, name="dp")
        nc.vector.scalar_tensor_tensor(cp[0][:, 0:H], c0[0][:, 0:H], 1.0, part[0][:, 0:H], ALU.mult, ALU.mult, accum_out=part[1][:, H : H + 1])
        nc.vector.scalar_tensor_tensor(late[:, 0:H], a[0][:, 0:H], aim_sb[:], part2[0][:, 0:H], ALU.subtract, ALU.mult)
        nc.vector.scalar_tensor_tensor(cp[1][:, 0 : H + 1], c0[1][:, 0 : H + 1], rz2[:], part[1][:, 0 : H + 1], ALU.mult, ALU.mult, accum_out=shift[:])
        nc.vector.scalar_tensor_tensor(late[:, H:I], a[1][:, 0:H], aim_sb[:], part2[1][:, 0:H], ALU.subtract, ALU.mult)
        nc.vector.tensor_scalar(dp[:, 0:H], c0[0][:, 0:H], neg_rz[:], shift[:], ALU.mult, ALU.add)
        nc.scalar.activation(dp[:, H:I], c0[1][:, 0:H], ACT.Identity, bias=shift[:], scale=neg_rz[:])
        nc.vector.tensor_tensor(placed[:].indirect(offsets[:]), dp[:], late[:, 0:I], ALU.mult)

        t0 = 0
        for n, width in enumerate(OUT_COLS):
            cols = slice(t0, t0 + width)
            res = sb.tile([P, width], F32, name="res%d" % n)
            nc.vector.tensor_tensor(res[:], placed[:, cols], old_sb[:, cols], ALU.add)
            (nc.sync if n % 2 == 0 else nc.scalar).dma_start(out=out[:, cols], in_=res[:])
            t0 += width
